import numpy as np
import ml_dtypes


def mxq(x, axis, fmt="e4m3"):
    dtype, down = {"e4m3": (ml_dtypes.float8_e4m3fn, 7), "e5m2": (ml_dtypes.float8_e5m2, 14)}[fmt]
    v = np.moveaxis(np.asarray(x, np.float32).astype(ml_dtypes.bfloat16).astype(np.float64), axis, -1)
    blocks = v.reshape(v.shape[:-1] + (-1, 32))
    amax = np.abs(blocks).max(-1, keepdims=True)
    byte = np.maximum(np.where(amax > 0, np.frexp(amax)[1] - 1 + 127, 0) - down, 1)
    scale = np.exp2(byte - 127.0)
    codes = (blocks / scale).astype(np.float32).astype(dtype).astype(np.float64)
    return np.moveaxis((codes * scale).reshape(v.shape), -1, axis)


WIDE = False


def mx_kscale(k):
    if not WIDE:
        return np.ones(k)
    levels = np.array([10, -10, 5, -5, 0])
    if k % 512:
        return np.exp2(np.random.permutation(np.resize(levels, k // 32))).repeat(32)
    a = np.empty((k // 512, 16))
    for p in range(k // 512):
        a[p, :8] = np.random.permutation(np.resize(levels, 8))
        for g in range(8):
            far = levels[np.abs(levels - a[p, g]) >= 10]
            a[p, g + 8] = far[np.random.randint(len(far))]
    return np.exp2(a.ravel()).repeat(32)


def f64(x):
    return np.asarray(x).astype(np.float64)


def striped8(idx):
    return np.asarray(idx).reshape(8, -1, 16).transpose(0, 2, 1).reshape(128, -1).astype(np.uint16)


def unstriped8(offs):
    return offs.reshape(8, 16, -1).transpose(0, 2, 1).reshape(8, -1).astype(np.int64)


def pick8(x, idx, run):
    r = np.arange(len(x))
    return x[r[:, None], idx[r % (8 * run) // run]]


E2M1 = np.array([0.0, 0.5, 1.0, 1.5, 2.0, 3.0, 4.0, 6.0, -0.0, -0.5, -1.0, -1.5, -2.0, -3.0, -4.0, -6.0])


def pack_weight(w, fmt):
    k, n = w.shape
    w = f64(np.asarray(w, np.float32).astype(ml_dtypes.bfloat16)).reshape(k // 32, 32, n)
    amax = np.abs(w).max(1)
    if fmt == "e4m3":
        byte = np.frexp(amax)[1] - 1 + 127 - 7
    else:
        mant, ex = np.frexp(amax / 6.0)
        byte = np.where(mant > 0.5, ex, ex - 1) + 127
    byte = np.clip(np.where(amax > 0, byte, 1), 1, 254)
    scaled = (w * np.exp2(127.0 - byte)[:, None, :]).reshape(k, n).astype(np.float32)
    by_word = np.ascontiguousarray(scaled.reshape(k // 512, 128, 4, n).transpose(0, 1, 3, 2))
    if fmt == "e4m3":
        words = by_word.astype(ml_dtypes.float8_e4m3fn).view(np.uint8)
    else:
        c = by_word.astype(ml_dtypes.float4_e2m1fn).view(np.uint8) & 0xF
        words = (c[..., 0::2] | (c[..., 1::2] << 4)).reshape(k // 512, 128, 2 * n)
    return np.ascontiguousarray(words), np.ascontiguousarray(byte.astype(np.uint8).reshape(k // 512, 16, n))


def unpack_weight(words, scales, fmt):
    g, _, n = scales.shape
    words = np.ascontiguousarray(words).reshape(g, 128, n, -1)
    if fmt == "e4m3":
        vals = words.view(ml_dtypes.float8_e4m3fn).astype(np.float64)
    else:
        nib = np.empty((g, 128, n, 4), np.uint8)
        nib[..., 0::2] = words & 0xF
        nib[..., 1::2] = words >> 4
        vals = E2M1[nib]
    vals = vals * np.repeat(np.exp2(scales.astype(np.float64) - 127.0), 8, axis=1)[..., None]
    return vals.transpose(0, 1, 3, 2).reshape(g * 512, n)


D, T, I, Q, E = 512, 1024, 512, 512, 256


def setup_inputs():
    n = np.random.standard_normal
    idx = np.stack([np.random.permutation(T)[:I] for _ in range(8)])
    idx2 = np.stack([np.random.permutation(T)[:I] for _ in range(8)])
    idx3 = np.stack([np.random.permutation(T)[:I] for _ in range(8)])
    idx4 = np.stack([np.random.permutation(T)[:I] for _ in range(8)])
    fd = mx_kscale(D)
    fq = mx_kscale(Q)
    cachep = pack_weight(n((D, T)) / fd[:, None], "e4m3")
    mixp = pack_weight(n((Q, E)) * 1.0 / np.sqrt(Q) / fq[:, None], "e2m1")
    return {
        "query": (n((D, Q)) * 1.0 / np.sqrt(D) * fd[:, None]).astype(np.float32),
        "cache_words": cachep[0],
        "cache_scales": cachep[1],
        "rowf": (np.random.uniform(0.5, 2.0, (Q, 1)) * fq[:, None]).astype(np.float32),
        "mix_words": mixp[0],
        "mix_scales": mixp[1],
        "offs": striped8(idx),
        "offs2": striped8(idx2),
        "offs3": striped8(idx3),
        "offs4": striped8(idx4),
    }


def reference(query, cache_words, cache_scales, rowf, mix_words, mix_scales, offs, offs2, offs3, offs4):
    idx = unstriped8(offs)
    idx2 = unstriped8(offs2)
    idx3 = unstriped8(offs3)
    idx4 = unstriped8(offs4)
    cacheu = unpack_weight(cache_words, cache_scales, "e4m3")
    mixu = unpack_weight(mix_words, mix_scales, "e2m1")
    queryq = mxq(f64(query), 0, "e4m3")
    a = queryq.T @ cacheu
    a1 = np.pad(a, ((0, 0), (512, 0)))[:, :T]
    f1 = np.zeros((Q, T))
    f1[np.arange(Q)[:, None], idx2[np.arange(Q) % 512 // 64]] = pick8(a1, idx, 64)
    c1 = np.maximum(a, f1)
    f2 = np.zeros((Q, T))
    f2[np.arange(Q)[:, None], idx4[np.arange(Q) % 512 // 64]] = pick8(c1, idx3, 64)
    c2 = c1 - f2
    g = pick8(c2, idx, 64)
    gw = g * f64(rowf)
    gwq = mxq(gw, 0, "e4m3")
    y = mixu.T @ gwq
    return y

@@ -1,0 +1,246 @@
+from contextlib import ExitStack
+
+import concourse.mybir as mybir
+
+D, T, I, Q, E = 512, 1024, 512, 512, 256
+FLOPS = 2 * D * Q * T + 2 * Q * E * I
+
+F32 = mybir.dt.float32
+BF16 = mybir.dt.bfloat16
+I32 = mybir.dt.int32
+U32 = mybir.dt.uint32
+U16 = mybir.dt.uint16
+U8 = mybir.dt.uint8
+FP8X4 = mybir.dt.float8_e4m3fn_x4
+FP4X4 = mybir.dt.float4_e2m1fn_x4
+COPY = mybir.ActivationFunctionType.Copy
+ALU = mybir.AluOpType
+
+P = 128
+PACK = 4
+HALF_T = T // 2
+HALF_I = I // 2
+HALF_Q = Q // 2
+LIST_COLS = I // 16
+
+
+def tile_attend_halfaway_one_mixed_kernel(
+    tc, query, cache_words, cache_scales, rowf, mix_words, mix_scales, offs, offs2, offs3, offs4, out
+):
+    nc = tc.nc
+    with ExitStack() as ctx:
+        sb = ctx.enter_context(tc.tile_pool(name="sb", bufs=1))
+        ps = ctx.enter_context(tc.psum_pool(name="ps", bufs=1))
+
+        def tile(shape, dtype, name):
+            return sb.tile(shape, dtype, name=name, align_bytes=64)
+
+        idx = sb.tile([P, LIST_COLS], U16, name="idx")
+        idx2 = sb.tile([P, LIST_COLS], U16, name="idx2")
+        idx3 = sb.tile([P, LIST_COLS], U16, name="idx3")
+        idx4 = sb.tile([P, LIST_COLS], U16, name="idx4")
+
+        def half_list(lst, u):
+            return lst[:, u * (LIST_COLS // 2) : (u + 1) * (LIST_COLS // 2)]
+
+        cache_sc = tile([P, T], U8, "cache_sc")
+        mix_sc = tile([P, E], U8, "mix_sc")
+        a1 = [tile([P, T], F32, "a1_%d" % b) for b in range(2)]
+        f1 = [tile([P, T], F32, "f1_%d" % b) for b in range(2)]
+        f2 = [tile([P, T], F32, "f2_%d" % b) for b in range(2)]
+
+        nc.vector.memset(cache_sc[:].bitcast(I32), 0)
+        nc.vector.memset(mix_sc[:].bitcast(I32), 0)
+        for b in range(2):
+            nc.vector.memset(a1[b][:, 0:HALF_T], 0.0)
+            nc.vector.memset(f1[b][:], 0.0)
+        for b in range(2):
+            nc.vector.memset(f2[b][:], 0.0)
+
+        raw = [tile([P, PACK, HALF_Q], F32, "raw%d" % c) for c in range(2)]
+        cache_w = [tile([P, HALF_T], U32, "cache_w%d" % h) for h in range(2)]
+        mix_w = tile([P, 2 * E], U8, "mix_w")
+        factor = tile([P, PACK], F32, "factor")
+        query_rows = query.rearrange("(p j) q -> p j q", j=PACK)
+        cache_rows = cache_words[0].rearrange("p n t -> p (n t)")
+
+        def load_cache_words(h):
+            src = cache_rows[:, h * HALF_T * PACK : (h + 1) * HALF_T * PACK]
+            nc.sync.dma_start(out=cache_w[h][:].bitcast(I32), in_=src.bitcast(I32))
+
+        def load_scale_rows(plane, rows):
+            for quad in range(4):
+                nc.sync.dma_start(
+                    out=plane[32 * quad : 32 * quad + 4, :].bitcast(I32),
+                    in_=rows[0, 4 * quad : 4 * quad + 4, :].bitcast(I32),
+                )
+
+        for c in range(2):
+            nc.sync.dma_start(out=raw[c][:], in_=query_rows[:, :, c * HALF_Q : (c + 1) * HALF_Q])
+        load_cache_words(0)
+        load_scale_rows(cache_sc, cache_scales)
+        nc.sync.dma_start(idx[:], offs)
+        nc.sync.dma_start(idx2[:], offs2)
+        load_cache_words(1)
+        nc.sync.dma_start(idx3[:], offs3)
+        nc.sync.dma_start(idx4[:], offs4)
+        nc.sync.dma_start(out=factor[:], in_=rowf.rearrange("(p r) o -> p (r o)", r=PACK))
+        nc.sync.dma_start(out=mix_w[:].bitcast(I32), in_=mix_words[0].bitcast(I32))
+        load_scale_rows(mix_sc, mix_scales)
+
+        q_first = tile([P, P, PACK], BF16, "q_first")
+        q_rest = tile([P, PACK - 1, P, PACK], BF16, "q_rest")
+        M = HALF_Q // PACK
+        for c in range(2):
+            nc.vector.tensor_copy(
+                out=q_first[:, c * M : (c + 1) * M, :],
+                in_=raw[c][:, :, 0:HALF_Q:PACK].rearrange("p j m -> p m j"),
+            )
+            nc.scalar.activation(
+                out=q_rest[:, :, c * M : (c + 1) * M, :].rearrange("p r m j -> p m r j"),
+                in_=raw[c][:].rearrange("p j (m r) -> p m r j", r=PACK)[:, :, 1:PACK, :],
+                func=COPY,
+            )
+        qw_first = tile([P, P], U32, "qw_first")
+        qs_first = tile([P, P], U8, "qs_first")
+        qw_rest = tile([P, (PACK - 1) * P], U32, "qw_rest")
+        qs_rest = tile([P, (PACK - 1) * P], U8, "qs_rest")
+        nc.vector.quantize_mx(
+            out=qw_first[:].bitcast(FP8X4), scales=qs_first[:], in_=q_first[:].rearrange("p m j -> p (m j)")
+        )
+
+        def scores(r, bank, t0, width):
+            if r == 0:
+                words, scales = qw_first[:], qs_first[:]
+            else:
+                words, scales = qw_rest[:, (r - 1) * P : r * P], qs_rest[:, (r - 1) * P : r * P]
+            acc = ps.tile([P, width], F32, name="a_%d_%d" % (r, t0), tag="bank%d" % bank)
+            h, c0 = divmod(t0, HALF_T)
+            nc.tensor.matmul_mx(
+                out=acc[:],
+                lhsT=words.bitcast(FP8X4),
+                lhsT_scale=scales,
+                rhs=cache_w[h][:, c0 : c0 + width].bitcast(FP8X4),
+                rhs_scale=cache_sc[:, t0 : t0 + width],
+                start=True,
+                stop=True,
+            )
+            return (acc, t0, width)
+
+        picked1 = [tile([P, I], F32, "picked1_%d" % r) for r in range(PACK)]
+        picked3 = [tile([P, I], F32, "picked3_%d" % r) for r in range(PACK)]
+        c1 = [tile([P, T], F32, "c1_%d" % r) for r in range(PACK)]
+        c2 = [tile([P, T], F32, "c2_%d" % b) for b in range(2)]
+        g = [tile([P, I], F32, "g_%d" % b) for b in range(2)]
+        gw = [tile([P, HALF_I, PACK], BF16, "gw_%d" % u) for u in range(2)]
+        last_pair = tile([P, 2, HALF_I], F32, "last_pair")
+
+        quarter = HALF_T // 2
+        a = {0: [scores(0, 0, 0, quarter), scores(0, 1, quarter, quarter)]}
+        nc.vector.tensor_copy(out=a1[0][:, HALF_T : HALF_T + quarter], in_=a[0][0][0][:])
+        nc.scalar.activation(out=a1[0][:, HALF_T + quarter : T], in_=a[0][1][0][:], func=COPY)
+        for u in range(2):
+            slots = slice(u * HALF_I, (u + 1) * HALF_I)
+            nc.vector.tensor_copy(out=picked1[0][:, slots], in_=a1[0][:].indirect(half_list(idx, u)))
+            nc.scalar.activation(out=f1[0][:].indirect(half_list(idx2, u)), in_=picked1[0][:, slots], func=COPY)
+
+        nc.vector.quantize_mx(
+            out=qw_rest[:].bitcast(FP8X4), scales=qs_rest[:], in_=q_rest[:].rearrange("p r m j -> p (r m j)")
+        )
+        for r in range(1, PACK):
+            a[r] = [scores(r, 1 + r, 0, HALF_T)]
+        for r in range(PACK - 1):
+            a[r].append(scores(r, 5 + r, HALF_T, HALF_T))
+
+        def shift_and_place(r):
+            nc.vector.tensor_copy(out=a1[r % 2][:, HALF_T:T], in_=a[r][0][0][:])
+            nc.vector.tensor_copy(out=picked1[r][:], in_=a1[r % 2][:].indirect(idx[:]))
+
+        def place1(r):
+            nc.scalar.activation(out=f1[r % 2][:].indirect(idx2[:]), in_=picked1[r][:], func=COPY)
+
+        def larger_and_place(r):
+            for acc, t0, width in a[r]:
+                cols = slice(t0, t0 + width)
+                nc.vector.tensor_tensor(out=c1[r][:, cols], in0=acc[:], in1=f1[r % 2][:, cols], op=ALU.max)
+
+        def pick3(r):
+            nc.vector.tensor_copy(out=picked3[r][:], in_=c1[r][:].indirect(idx3[:]))
+
+        def place2(r):
+            nc.scalar.activation(out=f2[r % 2][:].indirect(idx4[:]), in_=picked3[r][:], func=COPY)
+
+        def take_off(r):
+            nc.vector.tensor_tensor(out=c2[r % 2][:], in0=c1[r][:], in1=f2[r % 2][:], op=ALU.subtract)
+
+        def weigh(dst, src, r):
+            nc.vector.tensor_scalar(out=dst, in0=src, scalar1=factor[:, r : r + 1], scalar2=None, op0=ALU.mult)
+
+        def pick_and_weigh(r):
+            for u in range(2):
+                slots = slice(u * HALF_I, (u + 1) * HALF_I)
+                nc.vector.tensor_copy(out=g[r % 2][:, slots], in_=c2[r % 2][:].indirect(half_list(idx, u)))
+            weigh(gw[0][:, :, r], g[r % 2][:, 0:HALF_I], r)
+            weigh(last_pair[:, 0, :] if r == 2 else gw[1][:, :, r], g[r % 2][:, HALF_I:I], r)
+
+        shift_and_place(1)
+        place1(1)
+        shift_and_place(2)
+        larger_and_place(0)
+        place1(2)
+        pick3(0)
+        place2(0)
+        a[3].append(scores(3, 0, HALF_T, HALF_T))
+        larger_and_place(1)
+        pick3(1)
+        place2(1)
+        shift_and_place(3)
+        place1(3)
+        larger_and_place(2)
+        pick3(2)
+        take_off(0)
+        place2(2)
+        pick_and_weigh(0)
+        take_off(1)
+        pick_and_weigh(1)
+        larger_and_place(3)
+        pick3(3)
+        place2(3)
+        take_off(2)
+        pick_and_weigh(2)
+        take_off(3)
+
+        last = PACK - 1
+        nc.vector.tensor_copy(out=g[last % 2][:, 0:HALF_I], in_=c2[last % 2][:].indirect(half_list(idx, 0)))
+        nc.scalar.activation(
+            out=last_pair[:, 1, :],
+            in_=c2[last % 2][:].indirect(half_list(idx, 1)),
+            func=COPY,
+            scale=factor[:, last : last + 1],
+        )
+        weigh(gw[0][:, :, last], g[last % 2][:, 0:HALF_I], last)
+        nc.scalar.activation(out=gw[1][:, :, 2:4], in_=last_pair[:].rearrange("p r i -> p i r"), func=COPY)
+
+        for u in range(2):
+            words = tile([P, HALF_I], U32, "gw_words%d" % u)
+            scales = tile([P, HALF_I], U8, "gw_scales%d" % u)
+            nc.vector.quantize_mx(
+                out=words[:].bitcast(FP8X4), scales=scales[:], in_=gw[u][:].rearrange("p i r -> p (i r)")
+            )
+            for h in range(E // P):
+                acc = ps.tile([P, HALF_I], F32, name="y_%d_%d" % (u, h), tag="bank%d" % (1 + 2 * u + h))
+                nc.tensor.matmul_mx(
+                    out=acc[:],
+                    lhsT=mix_w[:, 2 * P * h : 2 * P * (h + 1)].bitcast(FP4X4),
+                    lhsT_scale=mix_sc[:, P * h : P * (h + 1)],
+                    rhs=words[:].bitcast(FP8X4),
+                    rhs_scale=scales[:],
+                    start=True,
+                    stop=True,
+                )
+                y = tile([P, HALF_I], F32, "y_sb_%d_%d" % (u, h))
+                if u == 1 and h == 0:
+                    nc.vector.tensor_copy(out=y[:], in_=acc[:])
+                else:
+                    nc.scalar.activation(out=y[:], in_=acc[:], func=COPY)
+                nc.sync.dma_start(out=out[P * h : P * (h + 1), u * HALF_I : (u + 1) * HALF_I], in_=y[:])

@@ -20,7 +20,6 @@ P = 128
 PACK = 4
 HALF_T = T // 2
 HALF_I = I // 2
-HALF_Q = Q // 2
 LIST_COLS = I // 16
 
 
@@ -43,21 +42,25 @@ def tile_attend_halfaway_one_mixed_kernel(
         def half_list(lst, u):
             return lst[:, u * (LIST_COLS // 2) : (u + 1) * (LIST_COLS // 2)]
 
-        cache_sc = tile([P, T], U8, "cache_sc")
+        cache_sc = [tile([P, HALF_T], U8, "cache_sc%d" % h) for h in range(2)]
         mix_sc = tile([P, E], U8, "mix_sc")
-        a1 = [tile([P, T], F32, "a1_%d" % b) for b in range(2)]
+        a1 = [sb.tile([P, T], F32, name="a1_%d" % b, tag="window%d" % b) for b in range(2)]
         f1 = [tile([P, T], F32, "f1_%d" % b) for b in range(2)]
         f2 = [tile([P, T], F32, "f2_%d" % b) for b in range(2)]
 
-        nc.vector.memset(cache_sc[:].bitcast(I32), 0)
-        nc.vector.memset(mix_sc[:].bitcast(I32), 0)
-        for b in range(2):
-            nc.vector.memset(a1[b][:, 0:HALF_T], 0.0)
-            nc.vector.memset(f1[b][:], 0.0)
-        for b in range(2):
-            nc.vector.memset(f2[b][:], 0.0)
+        def clear_on_vector(t, width):
+            cut = width // 2 - 1
+            nc.vector.memset(t[:, 0:cut], 0.0)
+            nc.vector.memset(t[:, cut:width], 0.0)
 
-        raw = [tile([P, PACK, HALF_Q], F32, "raw%d" % c) for c in range(2)]
+        clear_on_vector(a1[0], HALF_T)
+        clear_on_vector(f1[0], T)
+        clear_on_vector(f1[1], T)
+        nc.gpsimd.memset(a1[1][:, 0:HALF_T], 0.0)
+        for b in range(2):
+            nc.gpsimd.memset(f2[b][:], 0.0)
+
+        raw = [tile([P, 2, Q], F32, "raw%d" % c) for c in range(2)]
         cache_w = [tile([P, HALF_T], U32, "cache_w%d" % h) for h in range(2)]
         mix_w = tile([P, 2 * E], U8, "mix_w")
         factor = tile([P, PACK], F32, "factor")
@@ -68,52 +71,49 @@ def tile_attend_halfaway_one_mixed_kernel(
             src = cache_rows[:, h * HALF_T * PACK : (h + 1) * HALF_T * PACK]
             nc.sync.dma_start(out=cache_w[h][:].bitcast(I32), in_=src.bitcast(I32))
 
-        def load_scale_rows(plane, rows):
+        def load_scale_rows(queue, plane, rows):
             for quad in range(4):
-                nc.sync.dma_start(
+                queue.dma_start(
                     out=plane[32 * quad : 32 * quad + 4, :].bitcast(I32),
-                    in_=rows[0, 4 * quad : 4 * quad + 4, :].bitcast(I32),
+                    in_=rows[4 * quad : 4 * quad + 4, :].bitcast(I32),
                 )
 
+        load_scale_rows(nc.scalar, cache_sc[0], cache_scales[0][:, 0:HALF_T])
         for c in range(2):
-            nc.sync.dma_start(out=raw[c][:], in_=query_rows[:, :, c * HALF_Q : (c + 1) * HALF_Q])
+            nc.sync.dma_start(out=raw[c][:], in_=query_rows[:, 2 * c : 2 * c + 2, :])
         load_cache_words(0)
-        load_scale_rows(cache_sc, cache_scales)
         nc.sync.dma_start(idx[:], offs)
         nc.sync.dma_start(idx2[:], offs2)
         load_cache_words(1)
+        load_scale_rows(nc.sync, cache_sc[1], cache_scales[0][:, HALF_T:T])
         nc.sync.dma_start(idx3[:], offs3)
         nc.sync.dma_start(idx4[:], offs4)
         nc.sync.dma_start(out=factor[:], in_=rowf.rearrange("(p r) o -> p (r o)", r=PACK))
         nc.sync.dma_start(out=mix_w[:].bitcast(I32), in_=mix_words[0].bitcast(I32))
-        load_scale_rows(mix_sc, mix_scales)
+        load_scale_rows(nc.sync, mix_sc, mix_scales[0])
 
-        q_first = tile([P, P, PACK], BF16, "q_first")
-        q_rest = tile([P, PACK - 1, P, PACK], BF16, "q_rest")
-        M = HALF_Q // PACK
+        groups = [(0, 1), (1, 2), (2, 4)]
+        q_bf = [tile([P, hi - lo, P, PACK], BF16, "q_bf%d" % lo) for lo, hi in groups]
+        q_w = [tile([P, (hi - lo) * P], U32, "q_w%d" % lo) for lo, hi in groups]
+        q_s = [tile([P, (hi - lo) * P], U8, "q_s%d" % lo) for lo, hi in groups]
         for c in range(2):
-            nc.vector.tensor_copy(
-                out=q_first[:, c * M : (c + 1) * M, :],
-                in_=raw[c][:, :, 0:HALF_Q:PACK].rearrange("p j m -> p m j"),
+            for n, (lo, hi) in enumerate(groups):
+                dst = q_bf[n][:, :, :, 2 * c : 2 * c + 2].rearrange("p r m j -> p m r j")
+                src = raw[c][:].rearrange("p j (m r) -> p m r j", r=PACK)[:, :, lo:hi, :]
+                if n == 0:
+                    nc.vector.tensor_copy(out=dst, in_=src)
+                else:
+                    nc.scalar.activation(out=dst, in_=src, func=COPY)
+
+        def quantise_query(n):
+            nc.vector.quantize_mx(
+                out=q_w[n][:].bitcast(FP8X4), scales=q_s[n][:], in_=q_bf[n][:].rearrange("p r m j -> p (r m j)")
             )
-            nc.scalar.activation(
-                out=q_rest[:, :, c * M : (c + 1) * M, :].rearrange("p r m j -> p m r j"),
-                in_=raw[c][:].rearrange("p j (m r) -> p m r j", r=PACK)[:, :, 1:PACK, :],
-                func=COPY,
-            )
-        qw_first = tile([P, P], U32, "qw_first")
-        qs_first = tile([P, P], U8, "qs_first")
-        qw_rest = tile([P, (PACK - 1) * P], U32, "qw_rest")
-        qs_rest = tile([P, (PACK - 1) * P], U8, "qs_rest")
-        nc.vector.quantize_mx(
-            out=qw_first[:].bitcast(FP8X4), scales=qs_first[:], in_=q_first[:].rearrange("p m j -> p (m j)")
-        )
 
         def scores(r, bank, t0, width):
-            if r == 0:
-                words, scales = qw_first[:], qs_first[:]
-            else:
-                words, scales = qw_rest[:, (r - 1) * P : r * P], qs_rest[:, (r - 1) * P : r * P]
+            n = min(r, len(groups) - 1)
+            cols = slice((r - groups[n][0]) * P, (r - groups[n][0] + 1) * P)
+            words, scales = q_w[n][:, cols], q_s[n][:, cols]
             acc = ps.tile([P, width], F32, name="a_%d_%d" % (r, t0), tag="bank%d" % bank)
             h, c0 = divmod(t0, HALF_T)
             nc.tensor.matmul_mx(
@@ -121,7 +121,7 @@ def tile_attend_halfaway_one_mixed_kernel(
                 lhsT=words.bitcast(FP8X4),
                 lhsT_scale=scales,
                 rhs=cache_w[h][:, c0 : c0 + width].bitcast(FP8X4),
-                rhs_scale=cache_sc[:, t0 : t0 + width],
+                rhs_scale=cache_sc[h][:, c0 : c0 + width],
                 start=True,
                 stop=True,
             )
@@ -129,37 +129,44 @@ def tile_attend_halfaway_one_mixed_kernel(
 
         picked1 = [tile([P, I], F32, "picked1_%d" % r) for r in range(PACK)]
         picked3 = [tile([P, I], F32, "picked3_%d" % r) for r in range(PACK)]
-        c1 = [tile([P, T], F32, "c1_%d" % r) for r in range(PACK)]
-        c2 = [tile([P, T], F32, "c2_%d" % b) for b in range(2)]
+        c2 = tile([P, T], F32, "c2")
         g = [tile([P, I], F32, "g_%d" % b) for b in range(2)]
-        gw = [tile([P, HALF_I, PACK], BF16, "gw_%d" % u) for u in range(2)]
+        gw_first = tile([P, HALF_I, PACK], BF16, "gw_first")
+        gw_second = tile([P, HALF_I, PACK], BF16, "gw_second")
+        gw = [gw_first, gw_second]
         last_pair = tile([P, 2, HALF_I], F32, "last_pair")
 
         quarter = HALF_T // 2
-        a = {0: [scores(0, 0, 0, quarter), scores(0, 1, quarter, quarter)]}
+        quantise_query(0)
+        quantise_query(1)
+        a = {0: [scores(0, 0, 0, quarter), scores(0, 1, quarter, quarter)], 1: [scores(1, 2, 0, HALF_T)]}
         nc.vector.tensor_copy(out=a1[0][:, HALF_T : HALF_T + quarter], in_=a[0][0][0][:])
         nc.scalar.activation(out=a1[0][:, HALF_T + quarter : T], in_=a[0][1][0][:], func=COPY)
+        nc.scalar.activation(out=a1[1][:, HALF_T:T], in_=a[1][0][0][:], func=COPY)
         for u in range(2):
             slots = slice(u * HALF_I, (u + 1) * HALF_I)
             nc.vector.tensor_copy(out=picked1[0][:, slots], in_=a1[0][:].indirect(half_list(idx, u)))
             nc.scalar.activation(out=f1[0][:].indirect(half_list(idx2, u)), in_=picked1[0][:, slots], func=COPY)
 
-        nc.vector.quantize_mx(
-            out=qw_rest[:].bitcast(FP8X4), scales=qs_rest[:], in_=q_rest[:].rearrange("p r m j -> p (r m j)")
-        )
-        for r in range(1, PACK):
+        quantise_query(2)
+        for r in range(2, PACK):
             a[r] = [scores(r, 1 + r, 0, HALF_T)]
         for r in range(PACK - 1):
             a[r].append(scores(r, 5 + r, HALF_T, HALF_T))
 
-        def shift_and_place(r):
+        def shift(r):
             nc.vector.tensor_copy(out=a1[r % 2][:, HALF_T:T], in_=a[r][0][0][:])
+
+        def pick1(r):
             nc.vector.tensor_copy(out=picked1[r][:], in_=a1[r % 2][:].indirect(idx[:]))
 
         def place1(r):
             nc.scalar.activation(out=f1[r % 2][:].indirect(idx2[:]), in_=picked1[r][:], func=COPY)
 
-        def larger_and_place(r):
+        c1 = {}
+
+        def larger(r):
+            c1[r] = sb.tile([P, T], F32, name="c1_%d" % r, tag="window%d" % (r % 3))
             for acc, t0, width in a[r]:
                 cols = slice(t0, t0 + width)
                 nc.vector.tensor_tensor(out=c1[r][:, cols], in0=acc[:], in1=f1[r % 2][:, cols], op=ALU.max)
@@ -171,76 +178,114 @@ def tile_attend_halfaway_one_mixed_kernel(
             nc.scalar.activation(out=f2[r % 2][:].indirect(idx4[:]), in_=picked3[r][:], func=COPY)
 
         def take_off(r):
-            nc.vector.tensor_tensor(out=c2[r % 2][:], in0=c1[r][:], in1=f2[r % 2][:], op=ALU.subtract)
+            nc.vector.tensor_tensor(out=c2[:], in0=c1[r][:], in1=f2[r % 2][:], op=ALU.subtract)
 
         def weigh(dst, src, r):
             nc.vector.tensor_scalar(out=dst, in0=src, scalar1=factor[:, r : r + 1], scalar2=None, op0=ALU.mult)
 
-        def pick_and_weigh(r):
+        def pick(r):
             for u in range(2):
                 slots = slice(u * HALF_I, (u + 1) * HALF_I)
-                nc.vector.tensor_copy(out=g[r % 2][:, slots], in_=c2[r % 2][:].indirect(half_list(idx, u)))
+                nc.vector.tensor_copy(out=g[r % 2][:, slots], in_=c2[:].indirect(half_list(idx, u)))
+
+        def weigh_first(r):
             weigh(gw[0][:, :, r], g[r % 2][:, 0:HALF_I], r)
+
+        def weigh_second(r):
             weigh(last_pair[:, 0, :] if r == 2 else gw[1][:, :, r], g[r % 2][:, HALF_I:I], r)
 
-        shift_and_place(1)
+        pick1(1)
         place1(1)
-        shift_and_place(2)
-        larger_and_place(0)
+        shift(2)
+        shift(3)
+        pick1(2)
+        larger(0)
         place1(2)
+        a[3].append(scores(3, 0, HALF_T, HALF_T))
+        pick1(3)
         pick3(0)
         place2(0)
-        a[3].append(scores(3, 0, HALF_T, HALF_T))
-        larger_and_place(1)
+        larger(1)
+        place1(3)
+        larger(2)
         pick3(1)
         place2(1)
-        shift_and_place(3)
-        place1(3)
-        larger_and_place(2)
         pick3(2)
         take_off(0)
         place2(2)
-        pick_and_weigh(0)
-        take_off(1)
-        pick_and_weigh(1)
-        larger_and_place(3)
+        pick(0)
+        larger(3)
+        weigh_first(0)
+        weigh_second(0)
         pick3(3)
+        take_off(1)
         place2(3)
+        pick(1)
+        weigh_first(1)
         take_off(2)
-        pick_and_weigh(2)
+        weigh_second(1)
+        pick(2)
+        weigh_first(2)
+        weigh_second(2)
         take_off(3)
 
         last = PACK - 1
-        nc.vector.tensor_copy(out=g[last % 2][:, 0:HALF_I], in_=c2[last % 2][:].indirect(half_list(idx, 0)))
+        nc.vector.tensor_copy(out=g[last % 2][:, 0:HALF_I], in_=c2[:].indirect(half_list(idx, 0)))
         nc.scalar.activation(
             out=last_pair[:, 1, :],
-            in_=c2[last % 2][:].indirect(half_list(idx, 1)),
+            in_=c2[:].indirect(half_list(idx, 1)),
             func=COPY,
             scale=factor[:, last : last + 1],
         )
-        weigh(gw[0][:, :, last], g[last % 2][:, 0:HALF_I], last)
-        nc.scalar.activation(out=gw[1][:, :, 2:4], in_=last_pair[:].rearrange("p r i -> p i r"), func=COPY)
-
-        for u in range(2):
-            words = tile([P, HALF_I], U32, "gw_words%d" % u)
-            scales = tile([P, HALF_I], U8, "gw_scales%d" % u)
-            nc.vector.quantize_mx(
-                out=words[:].bitcast(FP8X4), scales=scales[:], in_=gw[u][:].rearrange("p i r -> p (i r)")
+        eighth = HALF_I // 2
+        for v in range(2):
+            slots = slice(v * eighth, (v + 1) * eighth)
+            weigh(gw[0][:, slots, last], g[last % 2][:, slots], last)
+            nc.scalar.activation(
+                out=gw[1][:, slots, 2:4], in_=last_pair[:, :, slots].rearrange("p r i -> p i r"), func=COPY
             )
-            for h in range(E // P):
-                acc = ps.tile([P, HALF_I], F32, name="y_%d_%d" % (u, h), tag="bank%d" % (1 + 2 * u + h))
-                nc.tensor.matmul_mx(
-                    out=acc[:],
-                    lhsT=mix_w[:, 2 * P * h : 2 * P * (h + 1)].bitcast(FP4X4),
-                    lhsT_scale=mix_sc[:, P * h : P * (h + 1)],
-                    rhs=words[:].bitcast(FP8X4),
-                    rhs_scale=scales[:],
-                    start=True,
-                    stop=True,
-                )
-                y = tile([P, HALF_I], F32, "y_sb_%d_%d" % (u, h))
-                if u == 1 and h == 0:
+
+        out_rows = out.rearrange("(h p) i -> p h i", p=P)
+
+        def quantise_weights(src, i0, width):
+            words = tile([P, width], U32, "gw_words%d" % i0)
+            scales = tile([P, width], U8, "gw_scales%d" % i0)
+            nc.vector.quantize_mx(out=words[:].bitcast(FP8X4), scales=scales[:], in_=src.rearrange("p i r -> p (i r)"))
+            return words, scales
+
+        def mix(acc, h, words, scales):
+            nc.tensor.matmul_mx(
+                out=acc,
+                lhsT=mix_w[:, 2 * P * h : 2 * P * (h + 1)].bitcast(FP4X4),
+                lhsT_scale=mix_sc[:, P * h : P * (h + 1)],
+                rhs=words[:].bitcast(FP8X4),
+                rhs_scale=scales[:],
+                start=True,
+                stop=True,
+            )
+
+        for n in range(4):
+            i0 = n * eighth
+            u, v = divmod(n, 2)
+            words, scales = quantise_weights(gw[u][:, v * eighth : (v + 1) * eighth, :], i0, eighth)
+            if n < 3:
+                acc = ps.tile([P, 2, eighth], F32, name="y_%d" % n, tag="bank%d" % (1 + n))
+                for h in range(2):
+                    mix(acc[:, h, :], h, words, scales)
+                y = tile([P, 2, eighth], F32, "y_sb_%d" % n)
+                if n == 1:
                     nc.vector.tensor_copy(out=y[:], in_=acc[:])
                 else:
                     nc.scalar.activation(out=y[:], in_=acc[:], func=COPY)
-                nc.sync.dma_start(out=out[P * h : P * (h + 1), u * HALF_I : (u + 1) * HALF_I], in_=y[:])
+                nc.sync.dma_start(out=out_rows[:, :, i0 : i0 + eighth], in_=y[:])
+            else:
+                for h in range(2):
+                    acc = ps.tile([P, eighth], F32, name="y_end_%d" % h, tag="bank%d" % (4 + h))
+                    mix(acc[:], h, words, scales)
+                    y = tile([P, eighth], F32, "y_end_sb_%d" % h)
+                    if h == 0:
+                        nc.vector.tensor_copy(out=y[:], in_=acc[:])
+                        nc.sync.dma_start(out=out_rows[:, h, i0:I], in_=y[:])
+                    else:
+                        nc.scalar.activation(out=y[:], in_=acc[:], func=COPY)
+                        nc.scalar.dma_start(out=out_rows[:, h, i0:I], in_=y[:])

@@ -42,10 +42,10 @@ def tile_attend_halfaway_one_mixed_kernel(
         def half_list(lst, u):
             return lst[:, u * (LIST_COLS // 2) : (u + 1) * (LIST_COLS // 2)]
 
-        cache_sc = [tile([P, HALF_T], U8, "cache_sc%d" % h) for h in range(2)]
+        cache_sc = tile([P, T], U8, "cache_sc")
         mix_sc = tile([P, E], U8, "mix_sc")
         a1 = [sb.tile([P, T], F32, name="a1_%d" % b, tag="window%d" % b) for b in range(2)]
-        f1 = [tile([P, T], F32, "f1_%d" % b) for b in range(2)]
+        f1 = [sb.tile([P, T], F32, name="f1_%d" % b, tag="placed%d" % b) for b in range(2)]
         f2 = [tile([P, T], F32, "f2_%d" % b) for b in range(2)]
 
         def clear_on_vector(t, width):
@@ -78,42 +78,43 @@ def tile_attend_halfaway_one_mixed_kernel(
                     in_=rows[4 * quad : 4 * quad + 4, :].bitcast(I32),
                 )
 
-        load_scale_rows(nc.scalar, cache_sc[0], cache_scales[0][:, 0:HALF_T])
+        load_scale_rows(nc.scalar, cache_sc, cache_scales[0])
         for c in range(2):
             nc.sync.dma_start(out=raw[c][:], in_=query_rows[:, 2 * c : 2 * c + 2, :])
         load_cache_words(0)
         nc.sync.dma_start(idx[:], offs)
         nc.sync.dma_start(idx2[:], offs2)
         load_cache_words(1)
-        load_scale_rows(nc.sync, cache_sc[1], cache_scales[0][:, HALF_T:T])
         nc.sync.dma_start(idx3[:], offs3)
         nc.sync.dma_start(idx4[:], offs4)
         nc.sync.dma_start(out=factor[:], in_=rowf.rearrange("(p r) o -> p (r o)", r=PACK))
         nc.sync.dma_start(out=mix_w[:].bitcast(I32), in_=mix_words[0].bitcast(I32))
         load_scale_rows(nc.sync, mix_sc, mix_scales[0])
 
-        groups = [(0, 1), (1, 2), (2, 4)]
-        q_bf = [tile([P, hi - lo, P, PACK], BF16, "q_bf%d" % lo) for lo, hi in groups]
-        q_w = [tile([P, (hi - lo) * P], U32, "q_w%d" % lo) for lo, hi in groups]
-        q_s = [tile([P, (hi - lo) * P], U8, "q_s%d" % lo) for lo, hi in groups]
+        q_bf = [tile([P, 2, P, PACK], BF16, "q_bf%d" % n) for n in range(2)]
         for c in range(2):
-            for n, (lo, hi) in enumerate(groups):
+            for n in range(2):
                 dst = q_bf[n][:, :, :, 2 * c : 2 * c + 2].rearrange("p r m j -> p m r j")
-                src = raw[c][:].rearrange("p j (m r) -> p m r j", r=PACK)[:, :, lo:hi, :]
+                src = raw[c][:].rearrange("p j (m r) -> p m r j", r=PACK)[:, :, 2 * n : 2 * n + 2, :]
                 if n == 0:
                     nc.vector.tensor_copy(out=dst, in_=src)
                 else:
                     nc.scalar.activation(out=dst, in_=src, func=COPY)
 
-        def quantise_query(n):
+        q_mx = {}
+
+        def quantise_query(first, count):
+            words = tile([P, count * P], U32, "q_words%d" % first)
+            scales = tile([P, count * P], U8, "q_scales%d" % first)
+            src = q_bf[first // 2][:, first % 2 : first % 2 + count, :, :]
             nc.vector.quantize_mx(
-                out=q_w[n][:].bitcast(FP8X4), scales=q_s[n][:], in_=q_bf[n][:].rearrange("p r m j -> p (r m j)")
+                out=words[:].bitcast(FP8X4), scales=scales[:], in_=src.rearrange("p r m j -> p (r m j)")
             )
+            for k in range(count):
+                q_mx[first + k] = (words[:, k * P : (k + 1) * P], scales[:, k * P : (k + 1) * P])
 
         def scores(r, bank, t0, width):
-            n = min(r, len(groups) - 1)
-            cols = slice((r - groups[n][0]) * P, (r - groups[n][0] + 1) * P)
-            words, scales = q_w[n][:, cols], q_s[n][:, cols]
+            words, scales = q_mx[r]
             acc = ps.tile([P, width], F32, name="a_%d_%d" % (r, t0), tag="bank%d" % bank)
             h, c0 = divmod(t0, HALF_T)
             nc.tensor.matmul_mx(
@@ -121,7 +122,7 @@ def tile_attend_halfaway_one_mixed_kernel(
                 lhsT=words.bitcast(FP8X4),
                 lhsT_scale=scales,
                 rhs=cache_w[h][:, c0 : c0 + width].bitcast(FP8X4),
-                rhs_scale=cache_sc[h][:, c0 : c0 + width],
+                rhs_scale=cache_sc[:, t0 : t0 + width],
                 start=True,
                 stop=True,
             )
@@ -129,7 +130,6 @@ def tile_attend_halfaway_one_mixed_kernel(
 
         picked1 = [tile([P, I], F32, "picked1_%d" % r) for r in range(PACK)]
         picked3 = [tile([P, I], F32, "picked3_%d" % r) for r in range(PACK)]
-        c2 = tile([P, T], F32, "c2")
         g = [tile([P, I], F32, "g_%d" % b) for b in range(2)]
         gw_first = tile([P, HALF_I, PACK], BF16, "gw_first")
         gw_second = tile([P, HALF_I, PACK], BF16, "gw_second")
@@ -137,8 +137,8 @@ def tile_attend_halfaway_one_mixed_kernel(
         last_pair = tile([P, 2, HALF_I], F32, "last_pair")
 
         quarter = HALF_T // 2
-        quantise_query(0)
-        quantise_query(1)
+        quantise_query(0, 1)
+        quantise_query(1, 1)
         a = {0: [scores(0, 0, 0, quarter), scores(0, 1, quarter, quarter)], 1: [scores(1, 2, 0, HALF_T)]}
         nc.vector.tensor_copy(out=a1[0][:, HALF_T : HALF_T + quarter], in_=a[0][0][0][:])
         nc.scalar.activation(out=a1[0][:, HALF_T + quarter : T], in_=a[0][1][0][:], func=COPY)
@@ -148,7 +148,7 @@ def tile_attend_halfaway_one_mixed_kernel(
             nc.vector.tensor_copy(out=picked1[0][:, slots], in_=a1[0][:].indirect(half_list(idx, u)))
             nc.scalar.activation(out=f1[0][:].indirect(half_list(idx2, u)), in_=picked1[0][:, slots], func=COPY)
 
-        quantise_query(2)
+        quantise_query(2, 2)
         for r in range(2, PACK):
             a[r] = [scores(r, 1 + r, 0, HALF_T)]
         for r in range(PACK - 1):
@@ -177,8 +177,11 @@ def tile_attend_halfaway_one_mixed_kernel(
         def place2(r):
             nc.scalar.activation(out=f2[r % 2][:].indirect(idx4[:]), in_=picked3[r][:], func=COPY)
 
+        c2 = {}
+
         def take_off(r):
-            nc.vector.tensor_tensor(out=c2[:], in0=c1[r][:], in1=f2[r % 2][:], op=ALU.subtract)
+            c2[r] = sb.tile([P, T], F32, name="c2_%d" % r, tag="placed%d" % min(r, 1))
+            nc.vector.tensor_tensor(out=c2[r][:], in0=c1[r][:], in1=f2[r % 2][:], op=ALU.subtract)
 
         def weigh(dst, src, r):
             nc.vector.tensor_scalar(out=dst, in0=src, scalar1=factor[:, r : r + 1], scalar2=None, op0=ALU.mult)
@@ -186,7 +189,7 @@ def tile_attend_halfaway_one_mixed_kernel(
         def pick(r):
             for u in range(2):
                 slots = slice(u * HALF_I, (u + 1) * HALF_I)
-                nc.vector.tensor_copy(out=g[r % 2][:, slots], in_=c2[:].indirect(half_list(idx, u)))
+                nc.vector.tensor_copy(out=g[r % 2][:, slots], in_=c2[r][:].indirect(half_list(idx, u)))
 
         def weigh_first(r):
             weigh(gw[0][:, :, r], g[r % 2][:, 0:HALF_I], r)
@@ -214,8 +217,8 @@ def tile_attend_halfaway_one_mixed_kernel(
         take_off(0)
         place2(2)
         pick(0)
-        larger(3)
         weigh_first(0)
+        larger(3)
         weigh_second(0)
         pick3(3)
         take_off(1)
@@ -230,10 +233,10 @@ def tile_attend_halfaway_one_mixed_kernel(
         take_off(3)
 
         last = PACK - 1
-        nc.vector.tensor_copy(out=g[last % 2][:, 0:HALF_I], in_=c2[:].indirect(half_list(idx, 0)))
+        nc.vector.tensor_copy(out=g[last % 2][:, 0:HALF_I], in_=c2[last][:].indirect(half_list(idx, 0)))
         nc.scalar.activation(
             out=last_pair[:, 1, :],
-            in_=c2[:].indirect(half_list(idx, 1)),
+            in_=c2[last][:].indirect(half_list(idx, 1)),
             func=COPY,
             scale=factor[:, last : last + 1],
         )

@@ -46,19 +46,10 @@ def tile_attend_halfaway_one_mixed_kernel(
         mix_sc = tile([P, E], U8, "mix_sc")
         a1 = [sb.tile([P, T], F32, name="a1_%d" % b, tag="window%d" % b) for b in range(2)]
         f1 = [sb.tile([P, T], F32, name="f1_%d" % b, tag="placed%d" % b) for b in range(2)]
-        f2 = [tile([P, T], F32, "f2_%d" % b) for b in range(2)]
 
-        def clear_on_vector(t, width):
-            cut = width // 2 - 1
-            nc.vector.memset(t[:, 0:cut], 0.0)
-            nc.vector.memset(t[:, cut:width], 0.0)
-
-        clear_on_vector(a1[0], HALF_T)
-        clear_on_vector(f1[0], T)
-        clear_on_vector(f1[1], T)
-        nc.gpsimd.memset(a1[1][:, 0:HALF_T], 0.0)
         for b in range(2):
-            nc.gpsimd.memset(f2[b][:], 0.0)
+            nc.vector.memset(a1[b][:, 0:HALF_T].bitcast(I32), 0)
+            nc.vector.memset(f1[b][:].bitcast(I32), 0)
 
         raw = [tile([P, 2, Q], F32, "raw%d" % c) for c in range(2)]
         cache_w = [tile([P, HALF_T], U32, "cache_w%d" % h) for h in range(2)]
@@ -128,7 +119,7 @@ def tile_attend_halfaway_one_mixed_kernel(
             )
             return (acc, t0, width)
 
-        picked1 = [tile([P, I], F32, "picked1_%d" % r) for r in range(PACK)]
+        picked1 = [sb.tile([P, I], F32, name="picked1_%d" % r, tag="picked%d" % r) for r in range(PACK)]
         picked3 = [tile([P, I], F32, "picked3_%d" % r) for r in range(PACK)]
         g = [tile([P, I], F32, "g_%d" % b) for b in range(2)]
         gw_first = tile([P, HALF_I, PACK], BF16, "gw_first")
@@ -174,6 +165,12 @@ def tile_attend_halfaway_one_mixed_kernel(
         def pick3(r):
             nc.vector.tensor_copy(out=picked3[r][:], in_=c1[r][:].indirect(idx3[:]))
 
+        f2 = {}
+
+        def clear_f2(b):
+            f2[b] = sb.tile([P, T], F32, name="f2_%d" % b, tag="picked%d" % b)
+            nc.vector.memset(f2[b][:].bitcast(I32), 0)
+
         def place2(r):
             nc.scalar.activation(out=f2[r % 2][:].indirect(idx4[:]), in_=picked3[r][:], func=COPY)
 
@@ -207,9 +204,11 @@ def tile_attend_halfaway_one_mixed_kernel(
         a[3].append(scores(3, 0, HALF_T, HALF_T))
         pick1(3)
         pick3(0)
+        clear_f2(0)
         place2(0)
         larger(1)
         place1(3)
+        clear_f2(1)
         larger(2)
         pick3(1)
         place2(1)

from contextlib import ExitStack

import concourse.mybir as mybir

D, T, I, Q, E = 512, 1024, 512, 512, 256
FLOPS = 2 * D * Q * T + 2 * Q * E * I

F32 = mybir.dt.float32
BF16 = mybir.dt.bfloat16
I32 = mybir.dt.int32
U32 = mybir.dt.uint32
U16 = mybir.dt.uint16
U8 = mybir.dt.uint8
FP8X4 = mybir.dt.float8_e4m3fn_x4
FP4X4 = mybir.dt.float4_e2m1fn_x4
COPY = mybir.ActivationFunctionType.Copy
ALU = mybir.AluOpType

P = 128
PACK = 4
HALF_T = T // 2
HALF_I = I // 2
LIST_COLS = I // 16


def tile_attend_halfaway_one_mixed_kernel(
    tc, query, cache_words, cache_scales, rowf, mix_words, mix_scales, offs, offs2, offs3, offs4, out
):
    nc = tc.nc
    with ExitStack() as ctx:
        sb = ctx.enter_context(tc.tile_pool(name="sb", bufs=1))
        ps = ctx.enter_context(tc.psum_pool(name="ps", bufs=1))

        def tile(shape, dtype, name):
            return sb.tile(shape, dtype, name=name, align_bytes=64)

        idx = sb.tile([P, LIST_COLS], U16, name="idx")
        idx2 = sb.tile([P, LIST_COLS], U16, name="idx2")
        idx3 = sb.tile([P, LIST_COLS], U16, name="idx3")
        idx4 = sb.tile([P, LIST_COLS], U16, name="idx4")

        def half_list(lst, u):
            return lst[:, u * (LIST_COLS // 2) : (u + 1) * (LIST_COLS // 2)]

        cache_sc = tile([P, T], U8, "cache_sc")
        mix_sc = tile([P, E], U8, "mix_sc")
        a1 = [sb.tile([P, T], F32, name="a1_%d" % b, tag="window%d" % b) for b in range(2)]
        f1 = [sb.tile([P, T], F32, name="f1_%d" % b, tag="placed%d" % b) for b in range(2)]

        for b in range(2):
            nc.vector.memset(a1[b][:, 0:HALF_T].bitcast(I32), 0)
            nc.vector.memset(f1[b][:].bitcast(I32), 0)

        raw = [tile([P, 2, Q], F32, "raw%d" % c) for c in range(2)]
        cache_w = [tile([P, HALF_T], U32, "cache_w%d" % h) for h in range(2)]
        mix_w = tile([P, 2 * E], U8, "mix_w")
        factor = tile([P, PACK], F32, "factor")
        query_rows = query.rearrange("(p j) q -> p j q", j=PACK)
        cache_rows = cache_words[0].rearrange("p n t -> p (n t)")

        def load_cache_words(h):
            src = cache_rows[:, h * HALF_T * PACK : (h + 1) * HALF_T * PACK]
            nc.sync.dma_start(out=cache_w[h][:].bitcast(I32), in_=src.bitcast(I32))

        def load_scale_rows(queue, plane, rows):
            for quad in range(4):
                queue.dma_start(
                    out=plane[32 * quad : 32 * quad + 4, :].bitcast(I32),
                    in_=rows[4 * quad : 4 * quad + 4, :].bitcast(I32),
                )

        load_scale_rows(nc.scalar, cache_sc, cache_scales[0])
        for c in range(2):
            nc.sync.dma_start(out=raw[c][:], in_=query_rows[:, 2 * c : 2 * c + 2, :])
        load_cache_words(0)
        nc.sync.dma_start(idx[:], offs)
        nc.sync.dma_start(idx2[:], offs2)
        load_cache_words(1)
        nc.sync.dma_start(idx3[:], offs3)
        nc.sync.dma_start(idx4[:], offs4)
        nc.sync.dma_start(out=factor[:], in_=rowf.rearrange("(p r) o -> p (r o)", r=PACK))
        nc.sync.dma_start(out=mix_w[:].bitcast(I32), in_=mix_words[0].bitcast(I32))
        load_scale_rows(nc.sync, mix_sc, mix_scales[0])

        q_bf = [tile([P, 2, P, PACK], BF16, "q_bf%d" % n) for n in range(2)]
        for c in range(2):
            for n in range(2):
                dst = q_bf[n][:, :, :, 2 * c : 2 * c + 2].rearrange("p r m j -> p m r j")
                src = raw[c][:].rearrange("p j (m r) -> p m r j", r=PACK)[:, :, 2 * n : 2 * n + 2, :]
                if n == 0:
                    nc.vector.tensor_copy(out=dst, in_=src)
                else:
                    nc.scalar.activation(out=dst, in_=src, func=COPY)

        q_mx = {}

        def quantise_query(first, count):
            words = tile([P, count * P], U32, "q_words%d" % first)
            scales = tile([P, count * P], U8, "q_scales%d" % first)
            src = q_bf[first // 2][:, first % 2 : first % 2 + count, :, :]
            nc.vector.quantize_mx(
                out=words[:].bitcast(FP8X4), scales=scales[:], in_=src.rearrange("p r m j -> p (r m j)")
            )
            for k in range(count):
                q_mx[first + k] = (words[:, k * P : (k + 1) * P], scales[:, k * P : (k + 1) * P])

        def scores(r, bank, t0, width):
            words, scales = q_mx[r]
            acc = ps.tile([P, width], F32, name="a_%d_%d" % (r, t0), tag="bank%d" % bank)
            h, c0 = divmod(t0, HALF_T)
            nc.tensor.matmul_mx(
                out=acc[:],
                lhsT=words.bitcast(FP8X4),
                lhsT_scale=scales,
                rhs=cache_w[h][:, c0 : c0 + width].bitcast(FP8X4),
                rhs_scale=cache_sc[:, t0 : t0 + width],
                start=True,
                stop=True,
            )
            return (acc, t0, width)

        picked1 = [sb.tile([P, I], F32, name="picked1_%d" % r, tag="picked%d" % r) for r in range(PACK)]
        picked3 = [tile([P, I], F32, "picked3_%d" % r) for r in range(PACK)]
        g = [tile([P, I], F32, "g_%d" % b) for b in range(2)]
        gw_first = tile([P, HALF_I, PACK], BF16, "gw_first")
        gw_second = tile([P, HALF_I, PACK], BF16, "gw_second")
        gw = [gw_first, gw_second]
        last_pair = tile([P, 2, HALF_I], F32, "last_pair")

        quarter = HALF_T // 2
        quantise_query(0, 1)
        quantise_query(1, 1)
        a = {0: [scores(0, 0, 0, quarter), scores(0, 1, quarter, quarter)], 1: [scores(1, 2, 0, HALF_T)]}
        nc.vector.tensor_copy(out=a1[0][:, HALF_T : HALF_T + quarter], in_=a[0][0][0][:])
        nc.scalar.activation(out=a1[0][:, HALF_T + quarter : T], in_=a[0][1][0][:], func=COPY)
        nc.scalar.activation(out=a1[1][:, HALF_T:T], in_=a[1][0][0][:], func=COPY)
        for u in range(2):
            slots = slice(u * HALF_I, (u + 1) * HALF_I)
            nc.vector.tensor_copy(out=picked1[0][:, slots], in_=a1[0][:].indirect(half_list(idx, u)))
            nc.scalar.activation(out=f1[0][:].indirect(half_list(idx2, u)), in_=picked1[0][:, slots], func=COPY)

        quantise_query(2, 2)
        for r in range(2, PACK):
            a[r] = [scores(r, 1 + r, 0, HALF_T)]
        for r in range(PACK - 1):
            a[r].append(scores(r, 5 + r, HALF_T, HALF_T))

        def shift(r):
            nc.vector.tensor_copy(out=a1[r % 2][:, HALF_T:T], in_=a[r][0][0][:])

        def pick1(r):
            nc.vector.tensor_copy(out=picked1[r][:], in_=a1[r % 2][:].indirect(idx[:]))

        def place1(r):
            nc.scalar.activation(out=f1[r % 2][:].indirect(idx2[:]), in_=picked1[r][:], func=COPY)

        c1 = {}

        def larger(r):
            c1[r] = sb.tile([P, T], F32, name="c1_%d" % r, tag="window%d" % (r % 3))
            for acc, t0, width in a[r]:
                cols = slice(t0, t0 + width)
                nc.vector.tensor_tensor(out=c1[r][:, cols], in0=acc[:], in1=f1[r % 2][:, cols], op=ALU.max)

        def pick3(r):
            nc.vector.tensor_copy(out=picked3[r][:], in_=c1[r][:].indirect(idx3[:]))

        f2 = {}

        def clear_f2(b):
            f2[b] = sb.tile([P, T], F32, name="f2_%d" % b, tag="picked%d" % b)
            nc.vector.memset(f2[b][:].bitcast(I32), 0)

        def place2(r):
            nc.scalar.activation(out=f2[r % 2][:].indirect(idx4[:]), in_=picked3[r][:], func=COPY)

        c2 = {}

        def take_off(r):
            c2[r] = sb.tile([P, T], F32, name="c2_%d" % r, tag="placed%d" % min(r, 1))
            nc.vector.tensor_tensor(out=c2[r][:], in0=c1[r][:], in1=f2[r % 2][:], op=ALU.subtract)

        def weigh(dst, src, r):
            nc.vector.tensor_scalar(out=dst, in0=src, scalar1=factor[:, r : r + 1], scalar2=None, op0=ALU.mult)

        def pick(r):
            for u in range(2):
                slots = slice(u * HALF_I, (u + 1) * HALF_I)
                nc.vector.tensor_copy(out=g[r % 2][:, slots], in_=c2[r][:].indirect(half_list(idx, u)))

        def weigh_first(r):
            weigh(gw[0][:, :, r], g[r % 2][:, 0:HALF_I], r)

        def weigh_second(r):
            weigh(last_pair[:, 0, :] if r == 2 else gw[1][:, :, r], g[r % 2][:, HALF_I:I], r)

        pick1(1)
        place1(1)
        shift(2)
        shift(3)
        pick1(2)
        larger(0)
        place1(2)
        a[3].append(scores(3, 0, HALF_T, HALF_T))
        pick1(3)
        pick3(0)
        clear_f2(0)
        place2(0)
        larger(1)
        place1(3)
        clear_f2(1)
        larger(2)
        pick3(1)
        place2(1)
        pick3(2)
        take_off(0)
        place2(2)
        pick(0)
        weigh_first(0)
        larger(3)
        weigh_second(0)
        pick3(3)
        take_off(1)
        place2(3)
        pick(1)
        weigh_first(1)
        take_off(2)
        weigh_second(1)
        pick(2)
        weigh_first(2)
        weigh_second(2)
        take_off(3)

        last = PACK - 1
        nc.vector.tensor_copy(out=g[last % 2][:, 0:HALF_I], in_=c2[last][:].indirect(half_list(idx, 0)))
        nc.scalar.activation(
            out=last_pair[:, 1, :],
            in_=c2[last][:].indirect(half_list(idx, 1)),
            func=COPY,
            scale=factor[:, last : last + 1],
        )
        eighth = HALF_I // 2
        for v in range(2):
            slots = slice(v * eighth, (v + 1) * eighth)
            weigh(gw[0][:, slots, last], g[last % 2][:, slots], last)
            nc.scalar.activation(
                out=gw[1][:, slots, 2:4], in_=last_pair[:, :, slots].rearrange("p r i -> p i r"), func=COPY
            )

        out_rows = out.rearrange("(h p) i -> p h i", p=P)

        def quantise_weights(src, i0, width):
            words = tile([P, width], U32, "gw_words%d" % i0)
            scales = tile([P, width], U8, "gw_scales%d" % i0)
            nc.vector.quantize_mx(out=words[:].bitcast(FP8X4), scales=scales[:], in_=src.rearrange("p i r -> p (i r)"))
            return words, scales

        def mix(acc, h, words, scales):
            nc.tensor.matmul_mx(
                out=acc,
                lhsT=mix_w[:, 2 * P * h : 2 * P * (h + 1)].bitcast(FP4X4),
                lhsT_scale=mix_sc[:, P * h : P * (h + 1)],
                rhs=words[:].bitcast(FP8X4),
                rhs_scale=scales[:],
                start=True,
                stop=True,
            )

        for n in range(4):
            i0 = n * eighth
            u, v = divmod(n, 2)
            words, scales = quantise_weights(gw[u][:, v * eighth : (v + 1) * eighth, :], i0, eighth)
            if n < 3:
                acc = ps.tile([P, 2, eighth], F32, name="y_%d" % n, tag="bank%d" % (1 + n))
                for h in range(2):
                    mix(acc[:, h, :], h, words, scales)
                y = tile([P, 2, eighth], F32, "y_sb_%d" % n)
                if n == 1:
                    nc.vector.tensor_copy(out=y[:], in_=acc[:])
                else:
                    nc.scalar.activation(out=y[:], in_=acc[:], func=COPY)
                nc.sync.dma_start(out=out_rows[:, :, i0 : i0 + eighth], in_=y[:])
            else:
                for h in range(2):
                    acc = ps.tile([P, eighth], F32, name="y_end_%d" % h, tag="bank%d" % (4 + h))
                    mix(acc[:], h, words, scales)
                    y = tile([P, eighth], F32, "y_end_sb_%d" % h)
                    if h == 0:
                        nc.vector.tensor_copy(out=y[:], in_=acc[:])
                        nc.sync.dma_start(out=out_rows[:, h, i0:I], in_=y[:])
                    else:
                        nc.scalar.activation(out=y[:], in_=acc[:], func=COPY)
                        nc.scalar.dma_start(out=out_rows[:, h, i0:I], in_=y[:])
